import numpy as np
import ml_dtypes


def mxq(x, axis, fmt="e4m3"):
    dtype, down = {"e4m3": (ml_dtypes.float8_e4m3fn, 7), "e5m2": (ml_dtypes.float8_e5m2, 14)}[fmt]
    v = np.moveaxis(np.asarray(x, np.float32).astype(ml_dtypes.bfloat16).astype(np.float64), axis, -1)
    blocks = v.reshape(v.shape[:-1] + (-1, 32))
    amax = np.abs(blocks).max(-1, keepdims=True)
    byte = np.maximum(np.where(amax > 0, np.frexp(amax)[1] - 1 + 127, 0) - down, 1)
    scale = np.exp2(byte - 127.0)
    codes = (blocks / scale).astype(np.float32).astype(dtype).astype(np.float64)
    return np.moveaxis((codes * scale).reshape(v.shape), -1, axis)


WIDE = False


def mx_kscale(k):
    if not WIDE:
        return np.ones(k)
    levels = np.array([10, -10, 5, -5, 0])
    if k % 512:
        return np.exp2(np.random.permutation(np.resize(levels, k // 32))).repeat(32)
    a = np.empty((k // 512, 16))
    for p in range(k // 512):
        a[p, :8] = np.random.permutation(np.resize(levels, 8))
        for g in range(8):
            far = levels[np.abs(levels - a[p, g]) >= 10]
            a[p, g + 8] = far[np.random.randint(len(far))]
    return np.exp2(a.ravel()).repeat(32)


def f64(x):
    return np.asarray(x).astype(np.float64)


def striped(idx):
    return np.tile(idx.reshape(-1, 16).T, (8, 1)).astype(np.uint16)


def unstriped(offs):
    return offs[:16].T.reshape(-1).astype(np.int64)


def pack_weight(w):
    k, n = w.shape
    w = f64(np.asarray(w, np.float32).astype(ml_dtypes.bfloat16)).reshape(k // 32, 32, n)
    amax = np.abs(w).max(1)
    byte = np.clip(np.where(amax > 0, np.frexp(amax)[1] - 1 + 127 - 7, 1), 1, 254)
    scaled = (w * np.exp2(127.0 - byte)[:, None, :]).reshape(k, n).astype(np.float32)
    words = np.ascontiguousarray(scaled.reshape(k // 512, 128, 4, n).transpose(0, 1, 3, 2)).astype(ml_dtypes.float8_e4m3fn).view(np.uint8)
    return words, np.ascontiguousarray(byte.astype(np.uint8).reshape(k // 512, 16, n))


def unpack_weight(words, scales):
    g, p, n, _ = words.shape
    vals = np.ascontiguousarray(words).view(ml_dtypes.float8_e4m3fn).astype(np.float64) * np.repeat(np.exp2(scales.astype(np.float64) - 127.0), 8, axis=1)[..., None]
    return vals.transpose(0, 1, 3, 2).reshape(g * 512, n)


def sigmoid(v):
    return 1.0 / (1.0 + np.exp(-np.maximum(v, -700.0)))


K, T, S, N = 512, 4096, 1024, 256
P = 2 ** 7


def setup_inputs():
    n = np.random.standard_normal
    s = mx_kscale(K)[:, None]
    packed_xT = pack_weight(n((K, T)) * s)
    return {
        "x_words": packed_xT[0],
        "x_scales": packed_xT[1],
        "w1": (n((K, N)) / np.sqrt(K) / s).astype(np.float32),
        "w2": (n((K, N)) / np.sqrt(K) / s).astype(np.float32),
        "paid": (np.random.uniform(0.3, 2.0, (N, S))).astype(np.float32),
        "prior": (np.tile(np.random.uniform(1.0, 5.0, S), (P, 1))).astype(np.float32),
        "offs": striped(np.random.permutation(T)[:S]),
    }


def reference(x_words, x_scales, w1, w2, paid, prior, offs):
    xq = unpack_weight(x_words, x_scales)[:, unstriped(offs)]
    yp = mxq(f64(w2), 0, "e4m3").T @ xq
    cred = sigmoid(yp)
    yc = mxq(f64(w1), 0, "e4m3").T @ xq
    fac = 0.5 * (np.log(np.exp(yc) + 1.0)) + 1.0
    fac2 = fac * (np.pad(fac, ((0, 0), (0, 1)))[:, 1:])
    fac4 = np.maximum(fac2, fac2 * (np.pad(fac2, ((0, 0), (0, 2)))[:, 2:]))
    ult = f64(paid) * fac4
    return cred * ult + (-1.0 * cred + 1.0) * (f64(paid) + f64(prior)[:1] * (-1.0 * (f64(paid) / (ult + 0.1)) + 1.0))

@@ -1,0 +1,191 @@
+import math
+from contextlib import ExitStack
+
+import concourse.mybir as mybir
+from concourse.masks import make_identity
+
+K, T, S, N = 512, 4096, 1024, 256
+FLOPS = 2 * 2 * K * S * N
+
+F32 = mybir.dt.float32
+BF16 = mybir.dt.bfloat16
+I32 = mybir.dt.int32
+U32 = mybir.dt.uint32
+U16 = mybir.dt.uint16
+U8 = mybir.dt.uint8
+FP8X4 = mybir.dt.float8_e4m3fn_x4
+ALU = mybir.AluOpType
+ACT = mybir.ActivationFunctionType
+
+P = 128
+PACK = 4
+MB = N // P
+PIECE = 256
+JB = PIECE // P
+HALF = 512
+PAD = 8
+LN_FLOOR = 1e-18
+
+
+def tile_picked_ychnld_bf_p_kernel(tc, x_words, x_scales, w1, w2, paid, prior, offs, out):
+    nc = tc.nc
+    pieces = list(reversed(range(S // PIECE)))
+    halves = list(reversed(range(S // HALF)))
+
+    with ExitStack() as ctx:
+        keep = ctx.enter_context(tc.tile_pool(name="keep", bufs=1))
+        psum = ctx.enter_context(tc.psum_pool(name="psum", bufs=1))
+
+        ident = keep.tile([P, P], F32, name="ident")
+        make_identity(nc, ident[:])
+        offsets = keep.tile([P, S // 16], U16, name="offsets")
+        prior_rows = keep.tile([P, P], F32, name="prior_rows", tag="prior_then_words", align_bytes=64)
+        nc.sync.dma_start(prior_rows[:], prior.rearrange("r (b p) -> (r b) p", p=P)[0:P, :])
+        w2_raw = keep.tile([P, PACK, N], F32, name="w2_raw")
+        nc.sync.dma_start(w2_raw[:], w2.rearrange("(p t) n -> p t n", t=PACK))
+        nc.sync.dma_start(offsets[:], offs)
+        scale_table = keep.tile([P, T], U8, name="scale_table", tag="scales_then_paid", align_bytes=64)
+        nc.vector.memset(scale_table[:].bitcast(I32), 0)
+        for quad in range(4):
+            nc.sync.dma_start(
+                scale_table[32 * quad : 32 * quad + 4, :].bitcast(I32),
+                x_scales[0][4 * quad : 4 * quad + 4, :].bitcast(I32),
+            )
+        prior_t = psum.tile([P, P], F32, name="prior_t", tag="mix", bufs=4)
+        nc.tensor.transpose(prior_t[:], prior_rows[:], ident[:])
+        prior_col = keep.tile([P, S // P], F32, name="prior_col")
+        nc.vector.tensor_copy(prior_col[:], prior_t[:, 0 : S // P])
+        word_table = keep.tile([P, T], I32, name="word_table", tag="prior_then_words", align_bytes=64)
+        nc.sync.dma_start(word_table[:], x_words[0].rearrange("p n t -> p (n t)").bitcast(I32))
+
+        x_bytes, x_codes = {}, {}
+        for h in halves:
+            x_bytes[h] = keep.tile([P, HALF], U8, name="x_bytes%d" % h, align_bytes=64)
+            nc.vector.tensor_copy(x_bytes[h][:], scale_table[:].indirect(offsets[:, h * 32 : (h + 1) * 32]))
+
+        def quantise(raw, name, sign):
+            grouped = keep.tile([P, N, PACK], BF16, name=name + "_grouped", align_bytes=64)
+            nc.vector.tensor_scalar(grouped[:], raw.rearrange("p t n -> p n t"), sign, None, ALU.mult)
+            codes = keep.tile([P, N], U32, name=name + "_codes", align_bytes=64)
+            scales = keep.tile([P, N], U8, name=name + "_scales", align_bytes=64)
+            nc.vector.quantize_mx(out=codes[:].bitcast(FP8X4), scales=scales[:], in_=grouped[:].rearrange("p n t -> p (n t)"))
+            return codes, scales
+
+        w2_codes, w2_scales = quantise(w2_raw[:], "w2", 1.0)
+        late = keep.tile([P, PACK * N + MB * S], F32, name="late", tag="scales_then_paid", align_bytes=64)
+        w1_raw = late[:, 0 : PACK * N].rearrange("p (t n) -> p t n", t=PACK)
+        nc.sync.dma_start(w1_raw, w1.rearrange("(p t) n -> p t n", t=PACK))
+        paid_sb = late[:, PACK * N :].rearrange("p (b j) -> p b j", b=MB)
+        nc.sync.dma_start(paid_sb, paid.rearrange("(b p) j -> p b j", p=P))
+
+        for h in halves:
+            x_codes[h] = keep.tile([P, HALF], U32, name="x_codes%d" % h, align_bytes=64)
+            nc.vector.tensor_copy(x_codes[h][:], word_table[:].bitcast(U32).indirect(offsets[:, h * 32 : (h + 1) * 32]))
+        w1_codes, w1_scales = quantise(w1_raw, "w1", -1.0)
+
+        def x_cols(j0, width):
+            h, c0 = divmod(j0, HALF)
+            return x_codes[h][:, c0 : c0 + width].bitcast(FP8X4), x_bytes[h][:, c0 : c0 + width]
+
+        rest = {}
+        for i in pieces:
+            yp = psum.tile([P, JB, N], F32, name="yp", tag="mix", bufs=4)
+            for jb in range(JB):
+                codes, scales = x_cols(i * PIECE + jb * P, P)
+                nc.tensor.matmul_mx(out=yp[:, jb, :], lhsT=codes, lhsT_scale=scales, rhs=w2_codes[:].bitcast(FP8X4), rhs_scale=w2_scales[:], start=True, stop=True)
+            rest[i] = keep.tile([P, JB, N], F32, name="rest%d" % i)
+            nc.scalar.activation(rest[i][:], yp[:], ACT.Sigmoid, scale=-1.0)
+
+        z, sig, lnsig = {}, {}, {}
+        for i in pieces:
+            z[i] = psum.tile([P, MB, PIECE], F32, name="z", tag="z_u", bufs=4)
+            codes, scales = x_cols(i * PIECE, PIECE)
+            for mb in range(MB):
+                cols = slice(mb * P, (mb + 1) * P)
+                nc.tensor.matmul_mx(out=z[i][:, mb, :], lhsT=w1_codes[:, cols].bitcast(FP8X4), lhsT_scale=w1_scales[:, cols], rhs=codes, rhs_scale=scales, start=True, stop=True)
+            sig[i] = keep.tile([P, MB, PIECE], F32, name="sig%d" % i)
+            nc.scalar.activation(sig[i][:], z[i][:], ACT.Sigmoid)
+        for i in pieces:
+            lnsig[i] = keep.tile([P, MB, PIECE], F32, name="lnsig%d" % i)
+            nc.scalar.activation(lnsig[i][:], sig[i][:], ACT.Ln, scale=math.exp(-2.0), bias=LN_FLOOR)
+
+        neg_g = keep.tile([P, MB, S + PAD], F32, name="neg_g")
+        g2 = keep.tile([P, MB, S + PAD], F32, name="g2")
+        nc.gpsimd.memset(neg_g[:, :, S:], 0.0)
+        nc.gpsimd.memset(g2[:, :, S:], 0.0)
+        neg_u = {}
+        for i in pieces:
+            j0 = i * PIECE
+            nc.vector.scalar_tensor_tensor(neg_g[:, :, j0 : j0 + PIECE], z[i][:], -2.0, lnsig[i][:], ALU.add, ALU.min)
+        for i in pieces:
+            j0 = i * PIECE
+            nc.vector.tensor_tensor(g2[:, :, j0 : j0 + PIECE], neg_g[:, :, j0 : j0 + PIECE], neg_g[:, :, j0 + 1 : j0 + 1 + PIECE], ALU.mult)
+        g4 = {}
+        for i in pieces:
+            j0 = i * PIECE
+            g4[i] = keep.tile([P, MB, PIECE], F32, name="g4_%d" % i)
+            nc.vector.scalar_tensor_tensor(g4[i][:], g2[:, :, j0 + 2 : j0 + 2 + PIECE], 4.0, g2[:, :, j0 : j0 + PIECE], ALU.max, ALU.mult)
+        neg_ut, inv2 = {}, {}
+        for i in pieces:
+            j0 = i * PIECE
+            neg_u[i] = keep.tile([P, MB, PIECE], F32, name="neg_u%d" % i)
+            nc.vector.scalar_tensor_tensor(neg_u[i][:], g4[i][:], -1.0 / 16.0, paid_sb[:, :, j0 : j0 + PIECE], ALU.mult, ALU.mult)
+            neg_ut[i] = psum.tile([P, JB, N], F32, name="neg_ut", tag="z_u", bufs=4)
+            for jb in range(JB):
+                for mb in range(MB):
+                    nc.tensor.transpose(neg_ut[i][:, jb, mb * P : (mb + 1) * P], neg_u[i][:, mb, jb * P : (jb + 1) * P], ident[:])
+            sq = keep.tile([P, JB, N], F32, name="sq", bufs=2)
+            nc.scalar.activation(sq[:], neg_ut[i][:], ACT.Square, bias=-0.1)
+            inv = keep.tile([P, JB, N], F32, name="inv", bufs=2)
+            nc.scalar.activation(inv[:], sq[:], ACT.Abs_reciprocal_sqrt)
+            inv2[i] = keep.tile([P, JB, N], F32, name="inv2_%d" % i)
+            nc.scalar.activation(inv2[i][:], inv[:], ACT.Square)
+
+        out_rows = out.rearrange("(b p) j -> p b j", p=P)
+        coef, base = {}, {}
+        for i in pieces:
+            paid_t = psum.tile([P, JB, N], F32, name="paid_t", tag="mix", bufs=4)
+            for jb in range(JB):
+                j0 = i * PIECE + jb * P
+                for mb in range(MB):
+                    nc.tensor.transpose(paid_t[:, jb, mb * P : (mb + 1) * P], paid_sb[:, mb, j0 : j0 + P], ident[:])
+            coef[i] = keep.tile([P, JB, N], F32, name="coef%d" % i)
+            base[i] = keep.tile([P, JB, N], F32, name="base%d" % i)
+            for jb in range(JB):
+                q = prior_col[:, i * JB + jb : i * JB + jb + 1]
+                nc.vector.scalar_tensor_tensor(coef[i][:, jb, :], rest[i][:, jb, :], q, paid_t[:, jb, :], ALU.mult, ALU.mult)
+                nc.vector.scalar_tensor_tensor(base[i][:, jb, :], paid_t[:, jb, :], q, rest[i][:, jb, :], ALU.add, ALU.mult)
+
+        for i in pieces:
+            j0 = i * PIECE
+            num = keep.tile([P, JB, N], F32, name="num", bufs=2)
+            nc.vector.scalar_tensor_tensor(num[:], neg_ut[i][:], -0.1, coef[i][:], ALU.add, ALU.mult)
+            own = keep.tile([P, JB, N], F32, name="own", bufs=2)
+            nc.vector.scalar_tensor_tensor(own[:], rest[i][:], -1.0, neg_ut[i][:], ALU.add, ALU.mult)
+            pull = keep.tile([P, JB, N], F32, name="pull", bufs=2)
+            result = keep.tile([P, MB, PIECE], F32, name="result%d" % i)
+            terms = [base[i], own, pull]
+
+            def turn_back(dst, mb, jb):
+                for n, term in enumerate(terms):
+                    nc.tensor.matmul(dst, term[:, jb, mb * P : (mb + 1) * P], ident[:], start=(n == 0), stop=(n == len(terms) - 1), is_transpose=True)
+
+            if i != pieces[-1]:
+                nc.vector.tensor_tensor(pull[:], num[:], inv2[i][:], ALU.mult)
+                total = psum.tile([P, MB, PIECE], F32, name="total", tag="mix", bufs=4)
+                for mb in range(MB):
+                    for jb in range(JB):
+                        turn_back(total[:, mb, jb * P : (jb + 1) * P], mb, jb)
+                nc.scalar.copy(result[:], total[:])
+                nc.sync.dma_start(out_rows[:, :, j0 : j0 + PIECE], result[:])
+            else:
+                for jb in range(JB):
+                    cols = slice(jb * P, (jb + 1) * P)
+                    nc.vector.tensor_tensor(pull[:, jb, :], num[:, jb, :], inv2[i][:, jb, :], ALU.mult)
+                    low = psum.tile([P, P], F32, name="low", tag="mix", bufs=4)
+                    high = psum.tile([P, P], F32, name="high", tag="z_u", bufs=4)
+                    turn_back(low[:], 0, jb)
+                    turn_back(high[:], 1, jb)
+                    nc.scalar.copy(result[:, 0, cols], low[:])
+                    nc.vector.tensor_copy(result[:, 1, cols], high[:])
+                    nc.sync.dma_start(out_rows[:, :, j0 + jb * P : j0 + (jb + 1) * P], result[:, :, cols])

@@ -2,7 +2,6 @@ import math
 from contextlib import ExitStack
 
 import concourse.mybir as mybir
-from concourse.masks import make_identity
 
 K, T, S, N = 512, 4096, 1024, 256
 FLOPS = 2 * 2 * K * S * N
@@ -36,16 +35,22 @@ def tile_picked_ychnld_bf_p_kernel(tc, x_words, x_scales, w1, w2, paid, prior, o
         keep = ctx.enter_context(tc.tile_pool(name="keep", bufs=1))
         psum = ctx.enter_context(tc.psum_pool(name="psum", bufs=1))
 
-        ident = keep.tile([P, P], F32, name="ident")
-        make_identity(nc, ident[:])
-        offsets = keep.tile([P, S // 16], U16, name="offsets")
-        prior_rows = keep.tile([P, P], F32, name="prior_rows", tag="prior_then_words", align_bytes=64)
-        nc.sync.dma_start(prior_rows[:], prior.rearrange("r (b p) -> (r b) p", p=P)[0:P, :])
-        w2_raw = keep.tile([P, PACK, N], F32, name="w2_raw")
-        nc.sync.dma_start(w2_raw[:], w2.rearrange("(p t) n -> p t n", t=PACK))
-        nc.sync.dma_start(offsets[:], offs)
         scale_table = keep.tile([P, T], U8, name="scale_table", tag="scales_then_paid", align_bytes=64)
         nc.vector.memset(scale_table[:].bitcast(I32), 0)
+        neg_g = keep.tile([P, MB, S + PAD], F32, name="neg_g")
+        g2 = keep.tile([P, MB, S + PAD], F32, name="g2")
+        nc.gpsimd.memset(neg_g[:, :, S:], 0.0)
+        nc.gpsimd.memset(g2[:, :, S:], 0.0)
+        zeros = keep.tile([P, P], F32, name="zeros", tag="zeros_then_words", align_bytes=64)
+        nc.gpsimd.memset(zeros[:], 0.0)
+        ident = keep.tile([P, P], F32, name="ident")
+        nc.gpsimd.affine_select(out=ident[:], in_=zeros[:], compare_op=ALU.not_equal, fill=1.0, base=0, pattern=[[-1, P]], channel_multiplier=1)
+        offsets = keep.tile([P, S // 16], U16, name="offsets")
+        prior_rows = keep.tile([P, P], F32, name="prior_rows")
+        w2_raw = keep.tile([P, PACK, N], F32, name="w2_raw")
+        nc.sync.dma_start(w2_raw[:], w2.rearrange("(p t) n -> p t n", t=PACK))
+        nc.sync.dma_start(prior_rows[:], prior.rearrange("r (b p) -> (r b) p", p=P)[0:P, :])
+        nc.sync.dma_start(offsets[:], offs)
         for quad in range(4):
             nc.sync.dma_start(
                 scale_table[32 * quad : 32 * quad + 4, :].bitcast(I32),
@@ -55,7 +60,7 @@ def tile_picked_ychnld_bf_p_kernel(tc, x_words, x_scales, w1, w2, paid, prior, o
         nc.tensor.transpose(prior_t[:], prior_rows[:], ident[:])
         prior_col = keep.tile([P, S // P], F32, name="prior_col")
         nc.vector.tensor_copy(prior_col[:], prior_t[:, 0 : S // P])
-        word_table = keep.tile([P, T], I32, name="word_table", tag="prior_then_words", align_bytes=64)
+        word_table = keep.tile([P, T], I32, name="word_table", tag="zeros_then_words", align_bytes=64)
         nc.sync.dma_start(word_table[:], x_words[0].rearrange("p n t -> p (n t)").bitcast(I32))
 
         x_bytes, x_codes = {}, {}
@@ -109,24 +114,22 @@ def tile_picked_ychnld_bf_p_kernel(tc, x_words, x_scales, w1, w2, paid, prior, o
             lnsig[i] = keep.tile([P, MB, PIECE], F32, name="lnsig%d" % i)
             nc.scalar.activation(lnsig[i][:], sig[i][:], ACT.Ln, scale=math.exp(-2.0), bias=LN_FLOOR)
 
-        neg_g = keep.tile([P, MB, S + PAD], F32, name="neg_g")
-        g2 = keep.tile([P, MB, S + PAD], F32, name="g2")
-        nc.gpsimd.memset(neg_g[:, :, S:], 0.0)
-        nc.gpsimd.memset(g2[:, :, S:], 0.0)
-        neg_u = {}
-        for i in pieces:
+        g4, neg_u, neg_ut, inv2 = {}, {}, {}, {}
+
+        def factor(i):
             j0 = i * PIECE
             nc.vector.scalar_tensor_tensor(neg_g[:, :, j0 : j0 + PIECE], z[i][:], -2.0, lnsig[i][:], ALU.add, ALU.min)
-        for i in pieces:
+
+        def pairs(i):
             j0 = i * PIECE
             nc.vector.tensor_tensor(g2[:, :, j0 : j0 + PIECE], neg_g[:, :, j0 : j0 + PIECE], neg_g[:, :, j0 + 1 : j0 + 1 + PIECE], ALU.mult)
-        g4 = {}
-        for i in pieces:
+
+        def fours(i):
             j0 = i * PIECE
             g4[i] = keep.tile([P, MB, PIECE], F32, name="g4_%d" % i)
             nc.vector.scalar_tensor_tensor(g4[i][:], g2[:, :, j0 + 2 : j0 + 2 + PIECE], 4.0, g2[:, :, j0 : j0 + PIECE], ALU.max, ALU.mult)
-        neg_ut, inv2 = {}, {}
-        for i in pieces:
+
+        def ultimate(i):
             j0 = i * PIECE
             neg_u[i] = keep.tile([P, MB, PIECE], F32, name="neg_u%d" % i)
             nc.vector.scalar_tensor_tensor(neg_u[i][:], g4[i][:], -1.0 / 16.0, paid_sb[:, :, j0 : j0 + PIECE], ALU.mult, ALU.mult)
@@ -134,15 +137,30 @@ def tile_picked_ychnld_bf_p_kernel(tc, x_words, x_scales, w1, w2, paid, prior, o
             for jb in range(JB):
                 for mb in range(MB):
                     nc.tensor.transpose(neg_ut[i][:, jb, mb * P : (mb + 1) * P], neg_u[i][:, mb, jb * P : (jb + 1) * P], ident[:])
-            sq = keep.tile([P, JB, N], F32, name="sq", bufs=2)
-            nc.scalar.activation(sq[:], neg_ut[i][:], ACT.Square, bias=-0.1)
+            root = keep.tile([P, JB, N], F32, name="root", bufs=2)
+            nc.scalar.activation(root[:], neg_ut[i][:], ACT.Abs_reciprocal_sqrt, bias=-0.1)
             inv = keep.tile([P, JB, N], F32, name="inv", bufs=2)
-            nc.scalar.activation(inv[:], sq[:], ACT.Abs_reciprocal_sqrt)
+            nc.scalar.activation(inv[:], root[:], ACT.Square)
             inv2[i] = keep.tile([P, JB, N], F32, name="inv2_%d" % i)
             nc.scalar.activation(inv2[i][:], inv[:], ACT.Square)
 
+        steps = [factor, pairs, fours, ultimate]
+        for tick in range(len(pieces) + len(steps) - 1):
+            for n in reversed(range(len(steps))):
+                if 0 <= tick - n < len(pieces):
+                    steps[n](pieces[tick - n])
+
         out_rows = out.rearrange("(b p) j -> p b j", p=P)
-        coef, base = {}, {}
+        coef, base, total = {}, {}, {}
+        last = pieces[-1]
+
+        def turn_back(dst, term, blocks, start, stop):
+            for n, jb in enumerate(blocks):
+                for mb in range(MB):
+                    nc.tensor.matmul(
+                        dst[:, mb, n * P : (n + 1) * P], term[:, jb, mb * P : (mb + 1) * P], ident[:],
+                        start=(start and n == 0 and mb == 0), stop=(stop and n == len(blocks) - 1 and mb == MB - 1), is_transpose=True)
+
         for i in pieces:
             paid_t = psum.tile([P, JB, N], F32, name="paid_t", tag="mix", bufs=4)
             for jb in range(JB):
@@ -156,36 +174,31 @@ def tile_picked_ychnld_bf_p_kernel(tc, x_words, x_scales, w1, w2, paid, prior, o
                 nc.vector.scalar_tensor_tensor(coef[i][:, jb, :], rest[i][:, jb, :], q, paid_t[:, jb, :], ALU.mult, ALU.mult)
                 nc.vector.scalar_tensor_tensor(base[i][:, jb, :], paid_t[:, jb, :], q, rest[i][:, jb, :], ALU.add, ALU.mult)
 
+        parts = [(i, [0, 1]) for i in pieces[:-1]] + [(last, [1]), (last, [0])]
+        for i, blocks in parts[:4]:
+            total[i, blocks[0]] = psum.tile([P, MB, len(blocks) * P], F32, name="total", tag="mix", bufs=4)
+            turn_back(total[i, blocks[0]], base[i], blocks, True, False)
+
+        num, own = {}, {}
         for i in pieces:
-            j0 = i * PIECE
-            num = keep.tile([P, JB, N], F32, name="num", bufs=2)
-            nc.vector.scalar_tensor_tensor(num[:], neg_ut[i][:], -0.1, coef[i][:], ALU.add, ALU.mult)
-            own = keep.tile([P, JB, N], F32, name="own", bufs=2)
-            nc.vector.scalar_tensor_tensor(own[:], rest[i][:], -1.0, neg_ut[i][:], ALU.add, ALU.mult)
-            pull = keep.tile([P, JB, N], F32, name="pull", bufs=2)
-            result = keep.tile([P, MB, PIECE], F32, name="result%d" % i)
-            terms = [base[i], own, pull]
-
-            def turn_back(dst, mb, jb):
-                for n, term in enumerate(terms):
-                    nc.tensor.matmul(dst, term[:, jb, mb * P : (mb + 1) * P], ident[:], start=(n == 0), stop=(n == len(terms) - 1), is_transpose=True)
-
-            if i != pieces[-1]:
-                nc.vector.tensor_tensor(pull[:], num[:], inv2[i][:], ALU.mult)
-                total = psum.tile([P, MB, PIECE], F32, name="total", tag="mix", bufs=4)
-                for mb in range(MB):
-                    for jb in range(JB):
-                        turn_back(total[:, mb, jb * P : (jb + 1) * P], mb, jb)
-                nc.scalar.copy(result[:], total[:])
-                nc.sync.dma_start(out_rows[:, :, j0 : j0 + PIECE], result[:])
-            else:
-                for jb in range(JB):
-                    cols = slice(jb * P, (jb + 1) * P)
-                    nc.vector.tensor_tensor(pull[:, jb, :], num[:, jb, :], inv2[i][:, jb, :], ALU.mult)
-                    low = psum.tile([P, P], F32, name="low", tag="mix", bufs=4)
-                    high = psum.tile([P, P], F32, name="high", tag="z_u", bufs=4)
-                    turn_back(low[:], 0, jb)
-                    turn_back(high[:], 1, jb)
-                    nc.scalar.copy(result[:, 0, cols], low[:])
-                    nc.vector.tensor_copy(result[:, 1, cols], high[:])
-                    nc.sync.dma_start(out_rows[:, :, j0 + jb * P : j0 + (jb + 1) * P], result[:, :, cols])
+            num[i] = keep.tile([P, JB, N], F32, name="num%d" % i)
+            nc.vector.scalar_tensor_tensor(num[i][:], neg_ut[i][:], -0.1, coef[i][:], ALU.add, ALU.mult)
+            own[i] = keep.tile([P, JB, N], F32, name="own%d" % i)
+            nc.vector.scalar_tensor_tensor(own[i][:], rest[i][:], -1.0, neg_ut[i][:], ALU.add, ALU.mult)
+            for pi, blocks in parts:
+                if pi != i:
+                    continue
+                if (i, blocks[0]) not in total:
+                    total[i, blocks[0]] = psum.tile([P, MB, len(blocks) * P], F32, name="total_last", tag="z_u", bufs=4)
+                    turn_back(total[i, blocks[0]], base[i], blocks, True, False)
+                acc = total[i, blocks[0]]
+                turn_back(acc, own[i], blocks, False, False)
+                rows = slice(blocks[0], blocks[-1] + 1)
+                pull = keep.tile([P, JB, N], F32, name="pull", bufs=3)
+                engine = nc.vector if i == last else nc.gpsimd
+                engine.tensor_tensor(pull[:, rows, :], num[i][:, rows, :], inv2[i][:, rows, :], ALU.mult)
+                turn_back(acc, pull, blocks, False, True)
+                result = keep.tile([P, MB, len(blocks) * P], F32, name="result%d_%d" % (i, blocks[0]))
+                nc.scalar.copy(result[:], acc[:])
+                j0 = i * PIECE + blocks[0] * P
+                nc.sync.dma_start(out_rows[:, :, j0 : j0 + len(blocks) * P], result[:])

@@ -24,6 +24,7 @@ JB = PIECE // P
 HALF = 512
 PAD = 8
 LN_FLOOR = 1e-18
+ZERO_SPLIT = 2560
 
 
 def tile_picked_ychnld_bf_p_kernel(tc, x_words, x_scales, w1, w2, paid, prior, offs, out):
@@ -36,15 +37,16 @@ def tile_picked_ychnld_bf_p_kernel(tc, x_words, x_scales, w1, w2, paid, prior, o
         psum = ctx.enter_context(tc.psum_pool(name="psum", bufs=1))
 
         scale_table = keep.tile([P, T], U8, name="scale_table", tag="scales_then_paid", align_bytes=64)
-        nc.vector.memset(scale_table[:].bitcast(I32), 0)
+        nc.gpsimd.memset(scale_table[:, 0:ZERO_SPLIT].bitcast(I32), 0)
+        nc.vector.memset(scale_table[:, ZERO_SPLIT:].bitcast(I32), 0)
         neg_g = keep.tile([P, MB, S + PAD], F32, name="neg_g")
         g2 = keep.tile([P, MB, S + PAD], F32, name="g2")
-        nc.gpsimd.memset(neg_g[:, :, S:], 0.0)
-        nc.gpsimd.memset(g2[:, :, S:], 0.0)
         zeros = keep.tile([P, P], F32, name="zeros", tag="zeros_then_words", align_bytes=64)
         nc.gpsimd.memset(zeros[:], 0.0)
         ident = keep.tile([P, P], F32, name="ident")
         nc.gpsimd.affine_select(out=ident[:], in_=zeros[:], compare_op=ALU.not_equal, fill=1.0, base=0, pattern=[[-1, P]], channel_multiplier=1)
+        nc.gpsimd.memset(neg_g[:, :, S:], 0.0)
+        nc.gpsimd.memset(g2[:, :, S:], 0.0)
         offsets = keep.tile([P, S // 16], U16, name="offsets")
         prior_rows = keep.tile([P, P], F32, name="prior_rows")
         w2_raw = keep.tile([P, PACK, N], F32, name="w2_raw")
@@ -70,7 +72,7 @@ def tile_picked_ychnld_bf_p_kernel(tc, x_words, x_scales, w1, w2, paid, prior, o
 
         def quantise(raw, name, sign):
             grouped = keep.tile([P, N, PACK], BF16, name=name + "_grouped", align_bytes=64)
-            nc.vector.tensor_scalar(grouped[:], raw.rearrange("p t n -> p n t"), sign, None, ALU.mult)
+            nc.vector.tensor_scalar(grouped[:].rearrange("p (c i) t -> p c t i", i=4), raw.rearrange("p t (c i) -> p c t i", i=4), sign, None, ALU.mult)
             codes = keep.tile([P, N], U32, name=name + "_codes", align_bytes=64)
             scales = keep.tile([P, N], U8, name=name + "_scales", align_bytes=64)
             nc.vector.quantize_mx(out=codes[:].bitcast(FP8X4), scales=scales[:], in_=grouped[:].rearrange("p n t -> p (n t)"))
@@ -80,8 +82,15 @@ def tile_picked_ychnld_bf_p_kernel(tc, x_words, x_scales, w1, w2, paid, prior, o
         late = keep.tile([P, PACK * N + MB * S], F32, name="late", tag="scales_then_paid", align_bytes=64)
         w1_raw = late[:, 0 : PACK * N].rearrange("p (t n) -> p t n", t=PACK)
         nc.sync.dma_start(w1_raw, w1.rearrange("(p t) n -> p t n", t=PACK))
-        paid_sb = late[:, PACK * N :].rearrange("p (b j) -> p b j", b=MB)
-        nc.sync.dma_start(paid_sb, paid.rearrange("(b p) j -> p b j", p=P))
+        paid_half = {}
+        for h in halves:
+            start = PACK * N + h * MB * HALF
+            paid_half[h] = late[:, start : start + MB * HALF].rearrange("p (b j) -> p b j", b=MB)
+            nc.sync.dma_start(paid_half[h], paid.rearrange("(b p) j -> p b j", p=P)[:, :, h * HALF : (h + 1) * HALF])
+
+        def paid_cols(j0, width):
+            h, c0 = divmod(j0, HALF)
+            return paid_half[h][:, :, c0 : c0 + width]
 
         for h in halves:
             x_codes[h] = keep.tile([P, HALF], U32, name="x_codes%d" % h, align_bytes=64)
@@ -132,7 +141,7 @@ def tile_picked_ychnld_bf_p_kernel(tc, x_words, x_scales, w1, w2, paid, prior, o
         def ultimate(i):
             j0 = i * PIECE
             neg_u[i] = keep.tile([P, MB, PIECE], F32, name="neg_u%d" % i)
-            nc.vector.scalar_tensor_tensor(neg_u[i][:], g4[i][:], -1.0 / 16.0, paid_sb[:, :, j0 : j0 + PIECE], ALU.mult, ALU.mult)
+            nc.vector.scalar_tensor_tensor(neg_u[i][:], g4[i][:], -1.0 / 16.0, paid_cols(j0, PIECE), ALU.mult, ALU.mult)
             neg_ut[i] = psum.tile([P, JB, N], F32, name="neg_ut", tag="z_u", bufs=4)
             for jb in range(JB):
                 for mb in range(MB):
@@ -166,7 +175,7 @@ def tile_picked_ychnld_bf_p_kernel(tc, x_words, x_scales, w1, w2, paid, prior, o
             for jb in range(JB):
                 j0 = i * PIECE + jb * P
                 for mb in range(MB):
-                    nc.tensor.transpose(paid_t[:, jb, mb * P : (mb + 1) * P], paid_sb[:, mb, j0 : j0 + P], ident[:])
+                    nc.tensor.transpose(paid_t[:, jb, mb * P : (mb + 1) * P], paid_cols(j0, P)[:, mb, :], ident[:])
             coef[i] = keep.tile([P, JB, N], F32, name="coef%d" % i)
             base[i] = keep.tile([P, JB, N], F32, name="base%d" % i)
             for jb in range(JB):
@@ -180,9 +189,12 @@ def tile_picked_ychnld_bf_p_kernel(tc, x_words, x_scales, w1, w2, paid, prior, o
             turn_back(total[i, blocks[0]], base[i], blocks, True, False)
 
         num, own = {}, {}
-        for i in pieces:
+
+        def numerator(i):
             num[i] = keep.tile([P, JB, N], F32, name="num%d" % i)
             nc.vector.scalar_tensor_tensor(num[i][:], neg_ut[i][:], -0.1, coef[i][:], ALU.add, ALU.mult)
+
+        def finish(i):
             own[i] = keep.tile([P, JB, N], F32, name="own%d" % i)
             nc.vector.scalar_tensor_tensor(own[i][:], rest[i][:], -1.0, neg_ut[i][:], ALU.add, ALU.mult)
             for pi, blocks in parts:
@@ -194,11 +206,24 @@ def tile_picked_ychnld_bf_p_kernel(tc, x_words, x_scales, w1, w2, paid, prior, o
                 acc = total[i, blocks[0]]
                 turn_back(acc, own[i], blocks, False, False)
                 rows = slice(blocks[0], blocks[-1] + 1)
-                pull = keep.tile([P, JB, N], F32, name="pull", bufs=3)
-                engine = nc.vector if i == last else nc.gpsimd
-                engine.tensor_tensor(pull[:, rows, :], num[i][:, rows, :], inv2[i][:, rows, :], ALU.mult)
-                turn_back(acc, pull, blocks, False, True)
+                pull = keep.tile([P, len(blocks), N], F32, name="pull%d_%d" % (i, blocks[0]))
+                if i == pieces[-2]:
+                    nc.gpsimd.tensor_tensor(pull[:, 1, :], num[i][:, 1, :], inv2[i][:, 1, :], ALU.mult)
+                    nc.vector.tensor_tensor(pull[:, 0, :], num[i][:, 0, :], inv2[i][:, 0, :], ALU.mult)
+                else:
+                    engine = nc.vector if i == last else nc.gpsimd
+                    engine.tensor_tensor(pull[:], num[i][:, rows, :], inv2[i][:, rows, :], ALU.mult)
+                turn_back(acc, pull, range(len(blocks)), False, True)
                 result = keep.tile([P, MB, len(blocks) * P], F32, name="result%d_%d" % (i, blocks[0]))
-                nc.scalar.copy(result[:], acc[:])
                 j0 = i * PIECE + blocks[0] * P
+                if (i, blocks) == parts[-1]:
+                    nc.vector.tensor_copy(result[:], acc[:])
+                else:
+                    nc.scalar.copy(result[:], acc[:])
                 nc.sync.dma_start(out_rows[:, :, j0 : j0 + len(blocks) * P], result[:])
+
+        numerator(pieces[0])
+        for n, i in enumerate(pieces):
+            if n + 1 < len(pieces):
+                numerator(pieces[n + 1])
+            finish(i)

@@ -34,14 +34,15 @@ def tile_picked_ychnld_bf_p_kernel(tc, x_words, x_scales, w1, w2, paid, prior, o
 
     with ExitStack() as ctx:
         keep = ctx.enter_context(tc.tile_pool(name="keep", bufs=1))
+        staged = ctx.enter_context(tc.tile_pool(name="staged", bufs=1))
         psum = ctx.enter_context(tc.psum_pool(name="psum", bufs=1))
 
-        scale_table = keep.tile([P, T], U8, name="scale_table", tag="scales_then_paid", align_bytes=64)
+        scale_table = keep.tile([P, T], U8, name="scale_table", align_bytes=64)
         nc.gpsimd.memset(scale_table[:, 0:ZERO_SPLIT].bitcast(I32), 0)
         nc.vector.memset(scale_table[:, ZERO_SPLIT:].bitcast(I32), 0)
         neg_g = keep.tile([P, MB, S + PAD], F32, name="neg_g")
         g2 = keep.tile([P, MB, S + PAD], F32, name="g2")
-        zeros = keep.tile([P, P], F32, name="zeros", tag="zeros_then_words", align_bytes=64)
+        zeros = staged.tile([P, P], F32, name="zeros", offset=4 * T - 2 * P, align_bytes=64)
         nc.gpsimd.memset(zeros[:], 0.0)
         ident = keep.tile([P, P], F32, name="ident")
         nc.gpsimd.affine_select(out=ident[:], in_=zeros[:], compare_op=ALU.not_equal, fill=1.0, base=0, pattern=[[-1, P]], channel_multiplier=1)
@@ -62,7 +63,7 @@ def tile_picked_ychnld_bf_p_kernel(tc, x_words, x_scales, w1, w2, paid, prior, o
         nc.tensor.transpose(prior_t[:], prior_rows[:], ident[:])
         prior_col = keep.tile([P, S // P], F32, name="prior_col")
         nc.vector.tensor_copy(prior_col[:], prior_t[:, 0 : S // P])
-        word_table = keep.tile([P, T], I32, name="word_table", tag="zeros_then_words", align_bytes=64)
+        word_table = staged.tile([P, T], I32, name="word_table", offset=0, align_bytes=64)
         nc.sync.dma_start(word_table[:], x_words[0].rearrange("p n t -> p (n t)").bitcast(I32))
 
         x_bytes, x_codes = {}, {}
@@ -79,7 +80,7 @@ def tile_picked_ychnld_bf_p_kernel(tc, x_words, x_scales, w1, w2, paid, prior, o
             return codes, scales
 
         w2_codes, w2_scales = quantise(w2_raw[:], "w2", 1.0)
-        late = keep.tile([P, PACK * N + MB * S], F32, name="late", tag="scales_then_paid", align_bytes=64)
+        late = staged.tile([P, PACK * N + MB * S], F32, name="late", offset=4 * T, align_bytes=64)
         w1_raw = late[:, 0 : PACK * N].rearrange("p (t n) -> p t n", t=PACK)
         nc.sync.dma_start(w1_raw, w1.rearrange("(p t) n -> p t n", t=PACK))
         paid_half = {}

import math
from contextlib import ExitStack

import concourse.mybir as mybir

K, T, S, N = 512, 4096, 1024, 256
FLOPS = 2 * 2 * K * S * N

F32 = mybir.dt.float32
BF16 = mybir.dt.bfloat16
I32 = mybir.dt.int32
U32 = mybir.dt.uint32
U16 = mybir.dt.uint16
U8 = mybir.dt.uint8
FP8X4 = mybir.dt.float8_e4m3fn_x4
ALU = mybir.AluOpType
ACT = mybir.ActivationFunctionType

P = 128
PACK = 4
MB = N // P
PIECE = 256
JB = PIECE // P
HALF = 512
PAD = 8
LN_FLOOR = 1e-18
ZERO_SPLIT = 2560


def tile_picked_ychnld_bf_p_kernel(tc, x_words, x_scales, w1, w2, paid, prior, offs, out):
    nc = tc.nc
    pieces = list(reversed(range(S // PIECE)))
    halves = list(reversed(range(S // HALF)))

    with ExitStack() as ctx:
        keep = ctx.enter_context(tc.tile_pool(name="keep", bufs=1))
        staged = ctx.enter_context(tc.tile_pool(name="staged", bufs=1))
        psum = ctx.enter_context(tc.psum_pool(name="psum", bufs=1))

        scale_table = keep.tile([P, T], U8, name="scale_table", align_bytes=64)
        nc.gpsimd.memset(scale_table[:, 0:ZERO_SPLIT].bitcast(I32), 0)
        nc.vector.memset(scale_table[:, ZERO_SPLIT:].bitcast(I32), 0)
        neg_g = keep.tile([P, MB, S + PAD], F32, name="neg_g")
        g2 = keep.tile([P, MB, S + PAD], F32, name="g2")
        zeros = staged.tile([P, P], F32, name="zeros", offset=4 * T - 2 * P, align_bytes=64)
        nc.gpsimd.memset(zeros[:], 0.0)
        ident = keep.tile([P, P], F32, name="ident")
        nc.gpsimd.affine_select(out=ident[:], in_=zeros[:], compare_op=ALU.not_equal, fill=1.0, base=0, pattern=[[-1, P]], channel_multiplier=1)
        nc.gpsimd.memset(neg_g[:, :, S:], 0.0)
        nc.gpsimd.memset(g2[:, :, S:], 0.0)
        offsets = keep.tile([P, S // 16], U16, name="offsets")
        prior_rows = keep.tile([P, P], F32, name="prior_rows")
        w2_raw = keep.tile([P, PACK, N], F32, name="w2_raw")
        nc.sync.dma_start(w2_raw[:], w2.rearrange("(p t) n -> p t n", t=PACK))
        nc.sync.dma_start(prior_rows[:], prior.rearrange("r (b p) -> (r b) p", p=P)[0:P, :])
        nc.sync.dma_start(offsets[:], offs)
        for quad in range(4):
            nc.sync.dma_start(
                scale_table[32 * quad : 32 * quad + 4, :].bitcast(I32),
                x_scales[0][4 * quad : 4 * quad + 4, :].bitcast(I32),
            )
        prior_t = psum.tile([P, P], F32, name="prior_t", tag="mix", bufs=4)
        nc.tensor.transpose(prior_t[:], prior_rows[:], ident[:])
        prior_col = keep.tile([P, S // P], F32, name="prior_col")
        nc.vector.tensor_copy(prior_col[:], prior_t[:, 0 : S // P])
        word_table = staged.tile([P, T], I32, name="word_table", offset=0, align_bytes=64)
        nc.sync.dma_start(word_table[:], x_words[0].rearrange("p n t -> p (n t)").bitcast(I32))

        x_bytes, x_codes = {}, {}
        for h in halves:
            x_bytes[h] = keep.tile([P, HALF], U8, name="x_bytes%d" % h, align_bytes=64)
            nc.vector.tensor_copy(x_bytes[h][:], scale_table[:].indirect(offsets[:, h * 32 : (h + 1) * 32]))

        def quantise(raw, name, sign):
            grouped = keep.tile([P, N, PACK], BF16, name=name + "_grouped", align_bytes=64)
            nc.vector.tensor_scalar(grouped[:].rearrange("p (c i) t -> p c t i", i=4), raw.rearrange("p t (c i) -> p c t i", i=4), sign, None, ALU.mult)
            codes = keep.tile([P, N], U32, name=name + "_codes", align_bytes=64)
            scales = keep.tile([P, N], U8, name=name + "_scales", align_bytes=64)
            nc.vector.quantize_mx(out=codes[:].bitcast(FP8X4), scales=scales[:], in_=grouped[:].rearrange("p n t -> p (n t)"))
            return codes, scales

        w2_codes, w2_scales = quantise(w2_raw[:], "w2", 1.0)
        late = staged.tile([P, PACK * N + MB * S], F32, name="late", offset=4 * T, align_bytes=64)
        w1_raw = late[:, 0 : PACK * N].rearrange("p (t n) -> p t n", t=PACK)
        nc.sync.dma_start(w1_raw, w1.rearrange("(p t) n -> p t n", t=PACK))
        paid_half = {}
        for h in halves:
            start = PACK * N + h * MB * HALF
            paid_half[h] = late[:, start : start + MB * HALF].rearrange("p (b j) -> p b j", b=MB)
            nc.sync.dma_start(paid_half[h], paid.rearrange("(b p) j -> p b j", p=P)[:, :, h * HALF : (h + 1) * HALF])

        def paid_cols(j0, width):
            h, c0 = divmod(j0, HALF)
            return paid_half[h][:, :, c0 : c0 + width]

        for h in halves:
            x_codes[h] = keep.tile([P, HALF], U32, name="x_codes%d" % h, align_bytes=64)
            nc.vector.tensor_copy(x_codes[h][:], word_table[:].bitcast(U32).indirect(offsets[:, h * 32 : (h + 1) * 32]))
        w1_codes, w1_scales = quantise(w1_raw, "w1", -1.0)

        def x_cols(j0, width):
            h, c0 = divmod(j0, HALF)
            return x_codes[h][:, c0 : c0 + width].bitcast(FP8X4), x_bytes[h][:, c0 : c0 + width]

        rest = {}
        for i in pieces:
            yp = psum.tile([P, JB, N], F32, name="yp", tag="mix", bufs=4)
            for jb in range(JB):
                codes, scales = x_cols(i * PIECE + jb * P, P)
                nc.tensor.matmul_mx(out=yp[:, jb, :], lhsT=codes, lhsT_scale=scales, rhs=w2_codes[:].bitcast(FP8X4), rhs_scale=w2_scales[:], start=True, stop=True)
            rest[i] = keep.tile([P, JB, N], F32, name="rest%d" % i)
            nc.scalar.activation(rest[i][:], yp[:], ACT.Sigmoid, scale=-1.0)

        z, sig, lnsig = {}, {}, {}
        for i in pieces:
            z[i] = psum.tile([P, MB, PIECE], F32, name="z", tag="z_u", bufs=4)
            codes, scales = x_cols(i * PIECE, PIECE)
            for mb in range(MB):
                cols = slice(mb * P, (mb + 1) * P)
                nc.tensor.matmul_mx(out=z[i][:, mb, :], lhsT=w1_codes[:, cols].bitcast(FP8X4), lhsT_scale=w1_scales[:, cols], rhs=codes, rhs_scale=scales, start=True, stop=True)
            sig[i] = keep.tile([P, MB, PIECE], F32, name="sig%d" % i)
            nc.scalar.activation(sig[i][:], z[i][:], ACT.Sigmoid)
        for i in pieces:
            lnsig[i] = keep.tile([P, MB, PIECE], F32, name="lnsig%d" % i)
            nc.scalar.activation(lnsig[i][:], sig[i][:], ACT.Ln, scale=math.exp(-2.0), bias=LN_FLOOR)

        g4, neg_u, neg_ut, inv2 = {}, {}, {}, {}

        def factor(i):
            j0 = i * PIECE
            nc.vector.scalar_tensor_tensor(neg_g[:, :, j0 : j0 + PIECE], z[i][:], -2.0, lnsig[i][:], ALU.add, ALU.min)

        def pairs(i):
            j0 = i * PIECE
            nc.vector.tensor_tensor(g2[:, :, j0 : j0 + PIECE], neg_g[:, :, j0 : j0 + PIECE], neg_g[:, :, j0 + 1 : j0 + 1 + PIECE], ALU.mult)

        def fours(i):
            j0 = i * PIECE
            g4[i] = keep.tile([P, MB, PIECE], F32, name="g4_%d" % i)
            nc.vector.scalar_tensor_tensor(g4[i][:], g2[:, :, j0 + 2 : j0 + 2 + PIECE], 4.0, g2[:, :, j0 : j0 + PIECE], ALU.max, ALU.mult)

        def ultimate(i):
            j0 = i * PIECE
            neg_u[i] = keep.tile([P, MB, PIECE], F32, name="neg_u%d" % i)
            nc.vector.scalar_tensor_tensor(neg_u[i][:], g4[i][:], -1.0 / 16.0, paid_cols(j0, PIECE), ALU.mult, ALU.mult)
            neg_ut[i] = psum.tile([P, JB, N], F32, name="neg_ut", tag="z_u", bufs=4)
            for jb in range(JB):
                for mb in range(MB):
                    nc.tensor.transpose(neg_ut[i][:, jb, mb * P : (mb + 1) * P], neg_u[i][:, mb, jb * P : (jb + 1) * P], ident[:])
            root = keep.tile([P, JB, N], F32, name="root", bufs=2)
            nc.scalar.activation(root[:], neg_ut[i][:], ACT.Abs_reciprocal_sqrt, bias=-0.1)
            inv = keep.tile([P, JB, N], F32, name="inv", bufs=2)
            nc.scalar.activation(inv[:], root[:], ACT.Square)
            inv2[i] = keep.tile([P, JB, N], F32, name="inv2_%d" % i)
            nc.scalar.activation(inv2[i][:], inv[:], ACT.Square)

        steps = [factor, pairs, fours, ultimate]
        for tick in range(len(pieces) + len(steps) - 1):
            for n in reversed(range(len(steps))):
                if 0 <= tick - n < len(pieces):
                    steps[n](pieces[tick - n])

        out_rows = out.rearrange("(b p) j -> p b j", p=P)
        coef, base, total = {}, {}, {}
        last = pieces[-1]

        def turn_back(dst, term, blocks, start, stop):
            for n, jb in enumerate(blocks):
                for mb in range(MB):
                    nc.tensor.matmul(
                        dst[:, mb, n * P : (n + 1) * P], term[:, jb, mb * P : (mb + 1) * P], ident[:],
                        start=(start and n == 0 and mb == 0), stop=(stop and n == len(blocks) - 1 and mb == MB - 1), is_transpose=True)

        for i in pieces:
            paid_t = psum.tile([P, JB, N], F32, name="paid_t", tag="mix", bufs=4)
            for jb in range(JB):
                j0 = i * PIECE + jb * P
                for mb in range(MB):
                    nc.tensor.transpose(paid_t[:, jb, mb * P : (mb + 1) * P], paid_cols(j0, P)[:, mb, :], ident[:])
            coef[i] = keep.tile([P, JB, N], F32, name="coef%d" % i)
            base[i] = keep.tile([P, JB, N], F32, name="base%d" % i)
            for jb in range(JB):
                q = prior_col[:, i * JB + jb : i * JB + jb + 1]
                nc.vector.scalar_tensor_tensor(coef[i][:, jb, :], rest[i][:, jb, :], q, paid_t[:, jb, :], ALU.mult, ALU.mult)
                nc.vector.scalar_tensor_tensor(base[i][:, jb, :], paid_t[:, jb, :], q, rest[i][:, jb, :], ALU.add, ALU.mult)

        parts = [(i, [0, 1]) for i in pieces[:-1]] + [(last, [1]), (last, [0])]
        for i, blocks in parts[:4]:
            total[i, blocks[0]] = psum.tile([P, MB, len(blocks) * P], F32, name="total", tag="mix", bufs=4)
            turn_back(total[i, blocks[0]], base[i], blocks, True, False)

        num, own = {}, {}

        def numerator(i):
            num[i] = keep.tile([P, JB, N], F32, name="num%d" % i)
            nc.vector.scalar_tensor_tensor(num[i][:], neg_ut[i][:], -0.1, coef[i][:], ALU.add, ALU.mult)

        def finish(i):
            own[i] = keep.tile([P, JB, N], F32, name="own%d" % i)
            nc.vector.scalar_tensor_tensor(own[i][:], rest[i][:], -1.0, neg_ut[i][:], ALU.add, ALU.mult)
            for pi, blocks in parts:
                if pi != i:
                    continue
                if (i, blocks[0]) not in total:
                    total[i, blocks[0]] = psum.tile([P, MB, len(blocks) * P], F32, name="total_last", tag="z_u", bufs=4)
                    turn_back(total[i, blocks[0]], base[i], blocks, True, False)
                acc = total[i, blocks[0]]
                turn_back(acc, own[i], blocks, False, False)
                rows = slice(blocks[0], blocks[-1] + 1)
                pull = keep.tile([P, len(blocks), N], F32, name="pull%d_%d" % (i, blocks[0]))
                if i == pieces[-2]:
                    nc.gpsimd.tensor_tensor(pull[:, 1, :], num[i][:, 1, :], inv2[i][:, 1, :], ALU.mult)
                    nc.vector.tensor_tensor(pull[:, 0, :], num[i][:, 0, :], inv2[i][:, 0, :], ALU.mult)
                else:
                    engine = nc.vector if i == last else nc.gpsimd
                    engine.tensor_tensor(pull[:], num[i][:, rows, :], inv2[i][:, rows, :], ALU.mult)
                turn_back(acc, pull, range(len(blocks)), False, True)
                result = keep.tile([P, MB, len(blocks) * P], F32, name="result%d_%d" % (i, blocks[0]))
                j0 = i * PIECE + blocks[0] * P
                if (i, blocks) == parts[-1]:
                    nc.vector.tensor_copy(result[:], acc[:])
                else:
                    nc.scalar.copy(result[:], acc[:])
                nc.sync.dma_start(out_rows[:, :, j0 : j0 + len(blocks) * P], result[:])

        numerator(pieces[0])
        for n, i in enumerate(pieces):
            if n + 1 < len(pieces):
                numerator(pieces[n + 1])
            finish(i)
